import numpy as np
import ml_dtypes


def mxq(x, axis, fmt="e4m3"):
    dtype, down = {"e4m3": (ml_dtypes.float8_e4m3fn, 7), "e5m2": (ml_dtypes.float8_e5m2, 14)}[fmt]
    v = np.moveaxis(np.asarray(x, np.float32).astype(ml_dtypes.bfloat16).astype(np.float64), axis, -1)
    blocks = v.reshape(v.shape[:-1] + (-1, 32))
    amax = np.abs(blocks).max(-1, keepdims=True)
    byte = np.maximum(np.where(amax > 0, np.frexp(amax)[1] - 1 + 127, 0) - down, 1)
    scale = np.exp2(byte - 127.0)
    codes = (blocks / scale).astype(np.float32).astype(dtype).astype(np.float64)
    return np.moveaxis((codes * scale).reshape(v.shape), -1, axis)


WIDE = False


def mx_kscale(k, group=512):
    if not WIDE:
        return np.ones(k)
    levels = np.array([10, -10, 5, -5, 0])
    if group != 512:
        return np.exp2(np.random.permutation(np.resize(levels, k // group))).repeat(group)
    if k % 512:
        return np.exp2(np.random.permutation(np.resize(levels, k // 32))).repeat(32)
    a = np.empty((k // 512, 16))
    for p in range(k // 512):
        a[p, :8] = np.random.permutation(np.resize(levels, 8))
        for g in range(8):
            far = levels[np.abs(levels - a[p, g]) >= 10]
            a[p, g + 8] = far[np.random.randint(len(far))]
    return np.exp2(a.ravel()).repeat(32)


def f64(x):
    return np.asarray(x).astype(np.float64)


def striped(idx):
    return np.tile(np.asarray(idx).reshape(-1, 16).T, (8, 1)).astype(np.uint16)


def unstriped(offs):
    return offs[:16].T.reshape(-1).astype(np.int64)


H, KV, D, NQ, N = 2, 2, 256, 512, 1024


def setup_inputs():
    n = np.random.standard_normal
    s = mx_kscale(D, 0)[:, None]
    u = mx_kscale(N)
    t = np.random.uniform(0.5, 2.0, N) * u
    v = n((KV, N, 128))
    v[:, :, 127] = 1.0
    return {
        "qT": (n((H, D, NQ)) * s * (0.70 / np.sqrt(D))).astype(np.float32),
        "kT": (n((KV, D, N)) / s).astype(np.float32),
        "t": t.reshape(N, 1).astype(np.float32),
        "v": (v / t[:, None]).astype(np.float32),
        "mask": (np.arange(N)[:, None] <= np.sort(np.random.randint(N // 4, N, NQ))[None, :]).astype(np.float32),
        "sink": (N * np.random.uniform(0.1, 1.0, (H, NQ, 1))).astype(np.float32),
        "og": n((H, NQ, 128)).astype(np.float32),
    }


def reference(qT, kT, t, v, mask, sink, og):
    a = mxq(f64(kT), 1, "e4m3").transpose(0, 2, 1) @ mxq(f64(qT), 1, "e4m3")
    p = np.exp(a)
    p = p * f64(mask)
    w = p * f64(t)
    y = mxq(w, 1, "e4m3").transpose(0, 2, 1) @ mxq(f64(v), 1, "e4m3")
    y = y / (y[:, :, 127:128] + f64(sink))
    y = y / (1.0 + np.exp(-f64(og)))
    return y

@@ -1,0 +1,199 @@
+from contextlib import ExitStack
+
+import concourse.mybir as mybir
+
+H, D, NQ, N, E = 2, 256, 512, 1024, 128
+FLOPS = 2 * H * N * NQ * D + 2 * H * N * NQ * E
+
+F32 = mybir.dt.float32
+BF16 = mybir.dt.bfloat16
+U32 = mybir.dt.uint32
+U8 = mybir.dt.uint8
+FP8X4 = mybir.dt.float8_e4m3fn_x4
+ACT = mybir.ActivationFunctionType
+ALU = mybir.AluOpType
+P = 128
+RUN = 2
+
+ORDER = "D:k0 D:qA D:k1 D:m0A D:qB D:m1A D:m0B D:v0 D:v1 D:m1B D:og D:sink S:k0d S:k0c V:k0a V:k0b V:qcA0 V:qcA1 V:kq0 V:qqA V:k1a V:k1b V:k1c V:mt0A0 V:mt0A1 P:m000 P:m001 P:m010 P:m011 S:e000 S:e001 S:k1d S:e010 S:e011 S:mt1A0 V:kq1 V:t000 V:qcB0 V:qcB1 V:t001 V:w000 V:t010 V:w001 V:qqB V:t011 V:w010 P:m100 P:m101 P:m110 P:m111 P:m020 P:m021 S:e100 S:mt1A1 S:e101 S:e110 S:mt0B0 S:e111 S:e020 S:vc00 S:e021 S:vc01 V:t100 V:w011 V:t101 V:w100 V:t110 V:w101 V:mt0B1 V:t111 V:w110 V:t020 V:w111 V:t021 V:w020 V:vq0 P:m030 P:m031 P:m120 P:m121 P:m130 P:m131 S:e030 S:vc10 S:e031 S:vc11 S:e120 S:e121 S:e130 S:e131 S:th S:g V:t030 V:w021 V:mt1B0 V:mt1B1 V:t031 V:w030 V:vq1 V:t120 V:w031 V:t121 V:w120 V:t130 V:w121 V:t131 V:w130 P:y0 P:y1 P:y2 V:d0 V:d1 V:w131 V:r0 V:r1 V:d2 V:o0 V:r2 D:st0 P:y3 V:d3 V:o1 V:r3 V:o2 V:o3 D:st1 D:st2 D:st3"
+
+
+def tile_rows_a_exp_mask_sink_gate_kernel(tc, qT, kT, t, v, mask, sink, og, out):
+    nc = tc.nc
+    with ExitStack() as ctx:
+        sb = ctx.enter_context(tc.tile_pool(name="sb", bufs=1))
+        ps = [ctx.enter_context(tc.psum_pool(name="ps%d" % h, bufs=3)) for h in range(H)]
+        psy = ctx.enter_context(tc.psum_pool(name="psy", bufs=1))
+        ctx.enter_context(nc.allow_non_contiguous_dma(reason="small per-partition columns"))
+        ctx.enter_context(tc.manual_schedule())
+
+        tiles = {}
+
+        def tl(name, shape, dtype):
+            if name not in tiles:
+                tiles[name] = sb.tile(shape, dtype, name=name, align_bytes=64)
+            return tiles[name]
+
+        ybank = [psy.tile([P, 4, E], F32, name="y%d" % b) for b in range(2)]
+        banks = {}
+        qv = qT.rearrange("h (p j) q -> (h p) j q", j=4)
+        kv = kT.rearrange("h (p j) n -> (h p) j n", j=4)
+
+        def cast(eng, dst, src):
+            if eng == "V":
+                nc.vector.tensor_copy(out=dst, in_=src)
+            else:
+                nc.scalar.copy(out=dst, in_=src)
+
+        def cast3(eng, dst, src):
+            if eng == "V":
+                nc.vector.tensor_copy(out=dst, in_=src)
+            else:
+                nc.scalar.activation(out=dst, in_=src, func=ACT.Copy)
+
+        def quant(name, src, words):
+            codes = tl(name + "c", [P, words], U32)
+            scales = tl(name + "s", [P, words], U8)
+            nc.vector.quantize_mx(out=codes[:].bitcast(FP8X4), scales=scales[:], in_=src)
+
+        t_sb = tl("t", [P, 2, 4], F32)
+        nc.scalar.dma_start(out=t_sb[:], in_=t.rearrange("(c p r) o -> p c (r o)", c=2, r=4))
+
+        def step(eng, n):
+            if eng == "D":
+                if n[0] == "k":
+                    c = int(n[1])
+                    nc.sync.dma_start(out=tl(n, [P, 4, 512], F32)[:], in_=kv[:, :, 512 * c : 512 * c + 512])
+                elif n[0] == "q":
+                    a = "AB".index(n[1])
+                    nc.sync.dma_start(out=tl(n, [P, 4, 256], F32)[:], in_=qv[:, :, 256 * a : 256 * a + 256])
+                elif n[0] == "m":
+                    c = int(n[1])
+                    a = "AB".index(n[2])
+                    src = mask[512 * c : 512 * c + 512, 256 * a : 256 * a + 256].rearrange("(p r) q -> p r q", r=4)
+                    nc.sync.dma_start(out=tl(n, [P, 4, 256], F32)[:], in_=src)
+                elif n[0] == "v":
+                    c = int(n[1])
+                    src = v[:, 512 * c : 512 * c + 512, :].rearrange("h (p r) e -> p h (r e)", r=4)
+                    nc.sync.dma_start(out=tl(n, [P, 2, 512], F32)[:], in_=src)
+                elif n == "og":
+                    nc.sync.dma_start(out=tl(n, [P, 8, E], F32)[:], in_=og.rearrange("h (b p) e -> p (h b) e", p=P))
+                elif n == "sink":
+                    nc.sync.dma_start(out=tl(n, [P, 2, 4], F32)[:], in_=sink.rearrange("h (b p) o -> p h (b o)", p=P))
+                else:
+                    b = int(n[2])
+                    dst = out[:, P * b : P * b + P, :].rearrange("h p e -> p h e")
+                    nc.sync.dma_start(out=dst, in_=tiles["o%d" % b][:])
+            elif n[0:2] == "kq":
+                quant(n, tiles["ks" + n[2]][:].rearrange("p r s j -> p (r s j)"), 512)
+            elif n[0] == "k":
+                i = "abcd".index(n[2])
+                st = tl("ks" + n[1], [P, 4, 128, 4], BF16)
+                src = tiles[n[0:2]][:, :, 128 * i : 128 * i + 128].rearrange("p j (s r) -> p s r j", r=4)
+                cast3(eng, st[:, :, 32 * i : 32 * i + 32, :].rearrange("p r s j -> p s r j"), src)
+            elif n[0:2] == "qc":
+                i = int(n[3])
+                st = tl("qs" + n[2], [P, 256, 4], BF16)
+                src = tiles["q" + n[2]][:, :, 128 * i : 128 * i + 128].rearrange("p j (c i) -> p c j i", i=RUN)
+                cast3(eng, st[:, 128 * i : 128 * i + 128, :].rearrange("p (c i) j -> p c j i", i=RUN), src)
+            elif n[0:2] == "qq":
+                quant(n, tiles["qs" + n[2]][:].rearrange("p q j -> p (q j)"), 256)
+            elif n[0:2] == "vc":
+                h = int(n[3])
+                st = tl("vs" + n[2], [P, 2, 128, 4], BF16)
+                src = tiles["v" + n[2]][:, h, :].rearrange("p (r c i) -> p c r i", r=4, i=RUN)
+                cast3(eng, st[:, h, :, :].rearrange("p (c i) r -> p c r i", i=RUN), src)
+            elif n[0:2] == "vq":
+                quant(n, tiles["vs" + n[2]][:].rearrange("p h e r -> p (h e r)"), 256)
+            elif n[0:2] == "mt":
+                c = int(n[2])
+                mt = tl(n[0:4], [P, 4, 256], F32)
+                m = tiles["m" + n[2:4]]
+                for r in (2 * int(n[4]), 2 * int(n[4]) + 1):
+                    if eng == "V":
+                        nc.vector.tensor_scalar(out=mt[:, r, :], in0=m[:, r, :], scalar1=t_sb[:, c, r : r + 1], scalar2=None, op0=ALU.mult)
+                    else:
+                        nc.scalar.activation(out=mt[:, r, :], in_=m[:, r, :], func=ACT.Copy, scale=t_sb[:, c, r : r + 1])
+            elif n == "th":
+                th = tl("th", [P, 8, E], F32)
+                nc.scalar.activation(out=th[:], in_=tiles["og"][:], func=ACT.Tanh, scale=0.5)
+            elif n == "g":
+                g = tl("g", [P, 8, E], F32)
+                if eng == "V":
+                    nc.vector.tensor_scalar(out=g[:], in0=tiles["th"][:], scalar1=0.5, scalar2=0.5, op0=ALU.mult, op1=ALU.add)
+                else:
+                    nc.scalar.activation(out=g[:], in_=tiles["th"][:], func=ACT.Copy, scale=0.5, bias=0.5)
+            elif n[0] == "m":
+                c, b, h = int(n[1]), int(n[2]), int(n[3])
+                bank = ps[h].tile([P, 4, 128], F32, name="sc%d" % h)
+                banks[n[1:]] = bank
+                rows = slice(64 * h, 64 * h + 64)
+                qn = "qq" + "AABB"[b]
+                qcols = slice(128 * (b % 2), 128 * (b % 2) + 128)
+                for r in range(4):
+                    kcols = slice(128 * r, 128 * r + 128)
+                    nc.tensor.matmul_mx(
+                        out=bank[:, r, :],
+                        lhsT=tiles["kq%dc" % c][rows, kcols].bitcast(FP8X4),
+                        lhsT_scale=tiles["kq%ds" % c][rows, kcols],
+                        rhs=tiles[qn + "c"][rows, qcols].bitcast(FP8X4),
+                        rhs_scale=tiles[qn + "s"][rows, qcols],
+                        start=True,
+                        stop=True,
+                    )
+            elif n[0] == "e":
+                p = tl("p" + n[1:], [P, 512], F32)
+                nc.scalar.activation(
+                    out=p[:].rearrange("p (c r i) -> p c r i", r=4, i=RUN),
+                    in_=banks[n[1:]][:].rearrange("p r (c i) -> p c r i", i=RUN),
+                    func=ACT.Exp,
+                )
+            elif n[0] == "t":
+                b = int(n[2])
+                w = tl("w" + n[1:], [P, 512], BF16)
+                mt = tiles["mt" + n[1] + "AABB"[b]]
+                nc.vector.tensor_tensor(
+                    out=w[:].rearrange("p (c i r) -> p c r i", r=4, i=RUN),
+                    in0=tiles["p" + n[1:]][:].rearrange("p (c r i) -> p c r i", r=4, i=RUN),
+                    in1=mt[:, :, 128 * (b % 2) : 128 * (b % 2) + 128].rearrange("p r (c i) -> p c r i", i=RUN),
+                    op=ALU.mult,
+                )
+            elif n[0] == "w":
+                quant("wq" + n[1:], tiles[n][:], 128)
+            elif n[0] == "y":
+                b = int(n[1])
+                for h in range(H):
+                    for c in range(2):
+                        u = "wq%d%d%d" % (c, b, h)
+                        vcols = slice(128 * h, 128 * h + 128)
+                        nc.tensor.matmul_mx(
+                            out=ybank[b % 2][:, 2 * (b // 2) + h, :],
+                            lhsT=tiles[u + "c"][:].bitcast(FP8X4),
+                            lhsT_scale=tiles[u + "s"][:],
+                            rhs=tiles["vq%dc" % c][:, vcols].bitcast(FP8X4),
+                            rhs_scale=tiles["vq%ds" % c][:, vcols],
+                            start=(c == 0),
+                            stop=(c == 1),
+                        )
+            elif n[0] == "d":
+                b = int(n[1])
+                d = tl(n, [P, 2], F32)
+                s0 = 2 * (b // 2)
+                nc.vector.tensor_tensor(out=d[:], in0=ybank[b % 2][:, s0 : s0 + 2, E - 1], in1=tiles["sink"][:, :, b], op=ALU.add)
+            elif n[0] == "r":
+                nc.vector.reciprocal(out=tl(n, [P, 2], F32)[:], in_=tiles["d" + n[1]][:])
+            else:
+                b = int(n[1])
+                o = tl(n, [P, 2, E], F32)
+                for h in range(H):
+                    nc.vector.scalar_tensor_tensor(
+                        out=o[:, h, :],
+                        in0=ybank[b % 2][:, 2 * (b // 2) + h, :],
+                        scalar=tiles["r%d" % b][:, h : h + 1],
+                        in1=tiles["g"][:, 4 * h + b, :],
+                        op0=ALU.mult,
+                        op1=ALU.mult,
+                    )
+
+        for item in ORDER.split():
+            step(item[0], item[2:])

@@ -2,8 +2,8 @@ from contextlib import ExitStack
 
 import concourse.mybir as mybir
 
-H, D, NQ, N, E = 2, 256, 512, 1024, 128
-FLOPS = 2 * H * N * NQ * D + 2 * H * N * NQ * E
+HEADS, FEATURES, QUERIES, TOKENS, VALUES = 2, 256, 512, 1024, 128
+FLOPS = 2 * HEADS * TOKENS * QUERIES * (FEATURES + VALUES)
 
 F32 = mybir.dt.float32
 BF16 = mybir.dt.bfloat16
@@ -12,188 +12,268 @@ U8 = mybir.dt.uint8
 FP8X4 = mybir.dt.float8_e4m3fn_x4
 ACT = mybir.ActivationFunctionType
 ALU = mybir.AluOpType
-P = 128
-RUN = 2
 
-ORDER = "D:k0 D:qA D:k1 D:m0A D:qB D:m1A D:m0B D:v0 D:v1 D:m1B D:og D:sink S:k0d S:k0c V:k0a V:k0b V:qcA0 V:qcA1 V:kq0 V:qqA V:k1a V:k1b V:k1c V:mt0A0 V:mt0A1 P:m000 P:m001 P:m010 P:m011 S:e000 S:e001 S:k1d S:e010 S:e011 S:mt1A0 V:kq1 V:t000 V:qcB0 V:qcB1 V:t001 V:w000 V:t010 V:w001 V:qqB V:t011 V:w010 P:m100 P:m101 P:m110 P:m111 P:m020 P:m021 S:e100 S:mt1A1 S:e101 S:e110 S:mt0B0 S:e111 S:e020 S:vc00 S:e021 S:vc01 V:t100 V:w011 V:t101 V:w100 V:t110 V:w101 V:mt0B1 V:t111 V:w110 V:t020 V:w111 V:t021 V:w020 V:vq0 P:m030 P:m031 P:m120 P:m121 P:m130 P:m131 S:e030 S:vc10 S:e031 S:vc11 S:e120 S:e121 S:e130 S:e131 S:th S:g V:t030 V:w021 V:mt1B0 V:mt1B1 V:t031 V:w030 V:vq1 V:t120 V:w031 V:t121 V:w120 V:t130 V:w121 V:t131 V:w130 P:y0 P:y1 P:y2 V:d0 V:d1 V:w131 V:r0 V:r1 V:d2 V:o0 V:r2 D:st0 P:y3 V:d3 V:o1 V:r3 V:o2 V:o3 D:st1 D:st2 D:st3"
+P = 128
+PACK = 4
+ROWS = FEATURES // PACK
+PASS = P * PACK
+PASSES = TOKENS // PASS
+BLOCK = 128
+BLOCKS = QUERIES // BLOCK
+RUN = 2
 
 
 def tile_rows_a_exp_mask_sink_gate_kernel(tc, qT, kT, t, v, mask, sink, og, out):
     nc = tc.nc
     with ExitStack() as ctx:
-        sb = ctx.enter_context(tc.tile_pool(name="sb", bufs=1))
-        ps = [ctx.enter_context(tc.psum_pool(name="ps%d" % h, bufs=3)) for h in range(H)]
-        psy = ctx.enter_context(tc.psum_pool(name="psy", bufs=1))
-        ctx.enter_context(nc.allow_non_contiguous_dma(reason="small per-partition columns"))
+        sbuf = ctx.enter_context(tc.tile_pool(name="sbuf", bufs=1))
+        score_pool = [ctx.enter_context(tc.psum_pool(name="scores%d" % h, bufs=2)) for h in range(HEADS)]
+        y_pool = ctx.enter_context(tc.psum_pool(name="y", bufs=1))
+        ctx.enter_context(nc.allow_non_contiguous_dma(reason="one sink a partition and head"))
         ctx.enter_context(tc.manual_schedule())
 
-        tiles = {}
+        def tiles(name, count, shape, dtype):
+            return [sbuf.tile(shape, dtype, name="%s%d" % (name, i), align_bytes=64) for i in range(count)]
 
-        def tl(name, shape, dtype):
-            if name not in tiles:
-                tiles[name] = sb.tile(shape, dtype, name=name, align_bytes=64)
-            return tiles[name]
+        def mx_tiles(name, count, words):
+            return list(zip(tiles(name + "_codes", count, [P, words], U32), tiles(name + "_scales", count, [P, words], U8)))
 
-        ybank = [psy.tile([P, 4, E], F32, name="y%d" % b) for b in range(2)]
-        banks = {}
-        qv = qT.rearrange("h (p j) q -> (h p) j q", j=4)
-        kv = kT.rearrange("h (p j) n -> (h p) j n", j=4)
+        def quantize(operand, source):
+            codes, scales = operand
+            nc.vector.quantize_mx(out=codes.bitcast(FP8X4), scales=scales, in_=source)
 
-        def cast(eng, dst, src):
-            if eng == "V":
-                nc.vector.tensor_copy(out=dst, in_=src)
-            else:
-                nc.scalar.copy(out=dst, in_=src)
+        def product(result, stationary, moving, start, stop):
+            nc.tensor.matmul_mx(
+                out=result,
+                lhsT=stationary[0].bitcast(FP8X4),
+                lhsT_scale=stationary[1],
+                rhs=moving[0].bitcast(FP8X4),
+                rhs_scale=moving[1],
+                start=start,
+                stop=stop,
+            )
 
-        def cast3(eng, dst, src):
-            if eng == "V":
-                nc.vector.tensor_copy(out=dst, in_=src)
-            else:
-                nc.scalar.activation(out=dst, in_=src, func=ACT.Copy)
+        def window(operand, rows, first, count):
+            return operand[0][rows, first : first + count], operand[1][rows, first : first + count]
 
-        def quant(name, src, words):
-            codes = tl(name + "c", [P, words], U32)
-            scales = tl(name + "s", [P, words], U8)
-            nc.vector.quantize_mx(out=codes[:].bitcast(FP8X4), scales=scales[:], in_=src)
+        def vector_round(dst, src):
+            nc.vector.tensor_copy(out=dst, in_=src)
 
-        t_sb = tl("t", [P, 2, 4], F32)
-        nc.scalar.dma_start(out=t_sb[:], in_=t.rearrange("(c p r) o -> p c (r o)", c=2, r=4))
+        def scalar_round(dst, src):
+            nc.scalar.activation(out=dst, in_=src, func=ACT.Copy)
 
-        def step(eng, n):
-            if eng == "D":
-                if n[0] == "k":
-                    c = int(n[1])
-                    nc.sync.dma_start(out=tl(n, [P, 4, 512], F32)[:], in_=kv[:, :, 512 * c : 512 * c + 512])
-                elif n[0] == "q":
-                    a = "AB".index(n[1])
-                    nc.sync.dma_start(out=tl(n, [P, 4, 256], F32)[:], in_=qv[:, :, 256 * a : 256 * a + 256])
-                elif n[0] == "m":
-                    c = int(n[1])
-                    a = "AB".index(n[2])
-                    src = mask[512 * c : 512 * c + 512, 256 * a : 256 * a + 256].rearrange("(p r) q -> p r q", r=4)
-                    nc.sync.dma_start(out=tl(n, [P, 4, 256], F32)[:], in_=src)
-                elif n[0] == "v":
-                    c = int(n[1])
-                    src = v[:, 512 * c : 512 * c + 512, :].rearrange("h (p r) e -> p h (r e)", r=4)
-                    nc.sync.dma_start(out=tl(n, [P, 2, 512], F32)[:], in_=src)
-                elif n == "og":
-                    nc.sync.dma_start(out=tl(n, [P, 8, E], F32)[:], in_=og.rearrange("h (b p) e -> p (h b) e", p=P))
-                elif n == "sink":
-                    nc.sync.dma_start(out=tl(n, [P, 2, 4], F32)[:], in_=sink.rearrange("h (b p) o -> p h (b o)", p=P))
-                else:
-                    b = int(n[2])
-                    dst = out[:, P * b : P * b + P, :].rearrange("h p e -> p h e")
-                    nc.sync.dma_start(out=dst, in_=tiles["o%d" % b][:])
-            elif n[0:2] == "kq":
-                quant(n, tiles["ks" + n[2]][:].rearrange("p r s j -> p (r s j)"), 512)
-            elif n[0] == "k":
-                i = "abcd".index(n[2])
-                st = tl("ks" + n[1], [P, 4, 128, 4], BF16)
-                src = tiles[n[0:2]][:, :, 128 * i : 128 * i + 128].rearrange("p j (s r) -> p s r j", r=4)
-                cast3(eng, st[:, :, 32 * i : 32 * i + 32, :].rearrange("p r s j -> p s r j"), src)
-            elif n[0:2] == "qc":
-                i = int(n[3])
-                st = tl("qs" + n[2], [P, 256, 4], BF16)
-                src = tiles["q" + n[2]][:, :, 128 * i : 128 * i + 128].rearrange("p j (c i) -> p c j i", i=RUN)
-                cast3(eng, st[:, 128 * i : 128 * i + 128, :].rearrange("p (c i) j -> p c j i", i=RUN), src)
-            elif n[0:2] == "qq":
-                quant(n, tiles["qs" + n[2]][:].rearrange("p q j -> p (q j)"), 256)
-            elif n[0:2] == "vc":
-                h = int(n[3])
-                st = tl("vs" + n[2], [P, 2, 128, 4], BF16)
-                src = tiles["v" + n[2]][:, h, :].rearrange("p (r c i) -> p c r i", r=4, i=RUN)
-                cast3(eng, st[:, h, :, :].rearrange("p (c i) r -> p c r i", i=RUN), src)
-            elif n[0:2] == "vq":
-                quant(n, tiles["vs" + n[2]][:].rearrange("p h e r -> p (h e r)"), 256)
-            elif n[0:2] == "mt":
-                c = int(n[2])
-                mt = tl(n[0:4], [P, 4, 256], F32)
-                m = tiles["m" + n[2:4]]
-                for r in (2 * int(n[4]), 2 * int(n[4]) + 1):
-                    if eng == "V":
-                        nc.vector.tensor_scalar(out=mt[:, r, :], in0=m[:, r, :], scalar1=t_sb[:, c, r : r + 1], scalar2=None, op0=ALU.mult)
-                    else:
-                        nc.scalar.activation(out=mt[:, r, :], in_=m[:, r, :], func=ACT.Copy, scale=t_sb[:, c, r : r + 1])
-            elif n == "th":
-                th = tl("th", [P, 8, E], F32)
-                nc.scalar.activation(out=th[:], in_=tiles["og"][:], func=ACT.Tanh, scale=0.5)
-            elif n == "g":
-                g = tl("g", [P, 8, E], F32)
-                if eng == "V":
-                    nc.vector.tensor_scalar(out=g[:], in0=tiles["th"][:], scalar1=0.5, scalar2=0.5, op0=ALU.mult, op1=ALU.add)
-                else:
-                    nc.scalar.activation(out=g[:], in_=tiles["th"][:], func=ACT.Copy, scale=0.5, bias=0.5)
-            elif n[0] == "m":
-                c, b, h = int(n[1]), int(n[2]), int(n[3])
-                bank = ps[h].tile([P, 4, 128], F32, name="sc%d" % h)
-                banks[n[1:]] = bank
-                rows = slice(64 * h, 64 * h + 64)
-                qn = "qq" + "AABB"[b]
-                qcols = slice(128 * (b % 2), 128 * (b % 2) + 128)
-                for r in range(4):
-                    kcols = slice(128 * r, 128 * r + 128)
-                    nc.tensor.matmul_mx(
-                        out=bank[:, r, :],
-                        lhsT=tiles["kq%dc" % c][rows, kcols].bitcast(FP8X4),
-                        lhsT_scale=tiles["kq%ds" % c][rows, kcols],
-                        rhs=tiles[qn + "c"][rows, qcols].bitcast(FP8X4),
-                        rhs_scale=tiles[qn + "s"][rows, qcols],
-                        start=True,
-                        stop=True,
-                    )
-            elif n[0] == "e":
-                p = tl("p" + n[1:], [P, 512], F32)
-                nc.scalar.activation(
-                    out=p[:].rearrange("p (c r i) -> p c r i", r=4, i=RUN),
-                    in_=banks[n[1:]][:].rearrange("p r (c i) -> p c r i", i=RUN),
-                    func=ACT.Exp,
-                )
-            elif n[0] == "t":
-                b = int(n[2])
-                w = tl("w" + n[1:], [P, 512], BF16)
-                mt = tiles["mt" + n[1] + "AABB"[b]]
-                nc.vector.tensor_tensor(
-                    out=w[:].rearrange("p (c i r) -> p c r i", r=4, i=RUN),
-                    in0=tiles["p" + n[1:]][:].rearrange("p (c r i) -> p c r i", r=4, i=RUN),
-                    in1=mt[:, :, 128 * (b % 2) : 128 * (b % 2) + 128].rearrange("p r (c i) -> p c r i", i=RUN),
-                    op=ALU.mult,
-                )
-            elif n[0] == "w":
-                quant("wq" + n[1:], tiles[n][:], 128)
-            elif n[0] == "y":
-                b = int(n[1])
-                for h in range(H):
-                    for c in range(2):
-                        u = "wq%d%d%d" % (c, b, h)
-                        vcols = slice(128 * h, 128 * h + 128)
-                        nc.tensor.matmul_mx(
-                            out=ybank[b % 2][:, 2 * (b // 2) + h, :],
-                            lhsT=tiles[u + "c"][:].bitcast(FP8X4),
-                            lhsT_scale=tiles[u + "s"][:],
-                            rhs=tiles["vq%dc" % c][:, vcols].bitcast(FP8X4),
-                            rhs_scale=tiles["vq%ds" % c][:, vcols],
-                            start=(c == 0),
-                            stop=(c == 1),
-                        )
-            elif n[0] == "d":
-                b = int(n[1])
-                d = tl(n, [P, 2], F32)
-                s0 = 2 * (b // 2)
-                nc.vector.tensor_tensor(out=d[:], in0=ybank[b % 2][:, s0 : s0 + 2, E - 1], in1=tiles["sink"][:, :, b], op=ALU.add)
-            elif n[0] == "r":
-                nc.vector.reciprocal(out=tl(n, [P, 2], F32)[:], in_=tiles["d" + n[1]][:])
-            else:
-                b = int(n[1])
-                o = tl(n, [P, 2, E], F32)
-                for h in range(H):
-                    nc.vector.scalar_tensor_tensor(
-                        out=o[:, h, :],
-                        in0=ybank[b % 2][:, 2 * (b // 2) + h, :],
-                        scalar=tiles["r%d" % b][:, h : h + 1],
-                        in1=tiles["g"][:, 4 * h + b, :],
-                        op0=ALU.mult,
-                        op1=ALU.mult,
-                    )
+        def vector_scale(dst, src, factor):
+            nc.vector.tensor_scalar(out=dst, in0=src, scalar1=factor, scalar2=None, op0=ALU.mult)
 
-        for item in ORDER.split():
-            step(item[0], item[2:])
+        def scalar_scale(dst, src, factor):
+            nc.scalar.activation(out=dst, in_=src, func=ACT.Copy, scale=factor)
+
+        everywhere = slice(0, P)
+        t_sb = tiles("t", 1, [P, PASSES, PACK], F32)[0]
+        q_raw = tiles("q_raw", 1, [P, PACK, QUERIES], F32)[0]
+        k_raw = tiles("k_raw", PASSES, [P, PACK, PASS], F32)
+        mask_raw = [tiles("mask_raw%d_" % c, 2, [P, 2, QUERIES], F32) for c in range(PASSES)]
+        v_raw = tiles("v_raw", PASSES, [P, HEADS, PACK * VALUES], F32)
+        og_sb = tiles("og", 1, [P, HEADS, BLOCKS, VALUES], F32)[0]
+        sink_sb = tiles("sink", 1, [P, HEADS, BLOCKS], F32)[0]
+
+        q_rows = qT.rearrange("h (p j) q -> (h p) j q", j=PACK)
+        k_rows = kT.rearrange("h (p j) n -> (h p) j n", j=PACK)
+        nc.scalar.dma_start(out=t_sb[:], in_=t.rearrange("(c p r) o -> p c (r o)", c=PASSES, r=PACK))
+        for c in range(PASSES):
+            tokens = slice(PASS * c, PASS * (c + 1))
+            nc.sync.dma_start(out=k_raw[c][:], in_=k_rows[:, :, tokens])
+            if c == 0:
+                nc.sync.dma_start(out=q_raw[:], in_=q_rows)
+            mask_rows = mask[tokens, :].rearrange("(p r) q -> p r q", r=PACK)
+            for pair in range(2):
+                nc.sync.dma_start(out=mask_raw[c][pair][:], in_=mask_rows[:, 2 * pair : 2 * pair + 2, :])
+        for c in range(PASSES):
+            tokens = slice(PASS * c, PASS * (c + 1))
+            nc.sync.dma_start(out=v_raw[c][:], in_=v[:, tokens, :].rearrange("h (p r) e -> p h (r e)", r=PACK))
+        nc.sync.dma_start(out=og_sb[:].rearrange("p h b e -> p (h b) e"), in_=og.rearrange("h (b p) e -> p (h b) e", p=P))
+        nc.sync.dma_start(out=sink_sb[:], in_=sink.rearrange("h (b p) o -> p h (b o)", p=P))
+
+        k_bf = [tiles("k_bf%d_" % c, 2, [P, 2, P, PACK], BF16) for c in range(PASSES)]
+        k_mx = [mx_tiles("k%d_" % c, 2, 2 * P) for c in range(PASSES)]
+        q_bf = tiles("q_bf", BLOCKS, [P, BLOCK, PACK], BF16)
+        q_mx = mx_tiles("q", BLOCKS, BLOCK)
+        v_bf = tiles("v_bf", PASSES, [P, HEADS, VALUES, PACK], BF16)
+        v_mx = mx_tiles("v", PASSES, HEADS * VALUES)
+        mask_t = tiles("mask_t", PASSES, [P, PACK, QUERIES], F32)
+        p_sb = [[tiles("p%d%d_" % (c, h), 2, [P, 2 * PASS], F32) for h in range(HEADS)] for c in range(PASSES)]
+        w_bf = [[tiles("w%d%d_" % (c, h), 2, [P, 2 * PASS], BF16) for h in range(HEADS)] for c in range(PASSES)]
+        w_mx = [[mx_tiles("w%d%d_" % (c, h), 2, 2 * BLOCK) for h in range(HEADS)] for c in range(PASSES)]
+        tanh_og = tiles("tanh_og", 1, [P, HEADS, BLOCKS, VALUES], F32)[0]
+        sink2 = tiles("sink2_", 1, [P, HEADS, BLOCKS], F32)[0]
+        den = tiles("den", BLOCKS, [P, HEADS], F32)
+        inv = tiles("inv", BLOCKS, [P, HEADS], F32)
+        gated = tiles("gated", BLOCKS, [P, HEADS, VALUES], F32)
+        result = tiles("result", BLOCKS, [P, HEADS, VALUES], F32)
+        y = [y_pool.tile([P, HEADS, VALUES], F32, name="y%d" % b) for b in range(BLOCKS)]
+
+        def round_keys(rounder, c, pair, first, last):
+            src = k_raw[c][:, :, PACK * first : PACK * last].rearrange("p j (s r) -> p s j r", r=PACK)
+            rounder(k_bf[c][pair][:, :, first:last, :].rearrange("p r s j -> p s j r"), src[:, :, :, 2 * pair : 2 * pair + 2])
+
+        def quantize_keys(c, pair):
+            quantize(window(k_mx[c][pair], everywhere, 0, 2 * P), k_bf[c][pair][:].rearrange("p r s j -> p (r s j)"))
+
+        def round_queries(rounder, b):
+            src = q_raw[:, :, BLOCK * b : BLOCK * (b + 1)].rearrange("p j (c i) -> p c j i", i=RUN)
+            rounder(q_bf[b][:].rearrange("p (c i) j -> p c j i", i=RUN), src)
+
+        def quantize_queries(b):
+            quantize(window(q_mx[b], everywhere, 0, BLOCK), q_bf[b][:].rearrange("p q j -> p (q j)"))
+
+        def round_values(c, h):
+            src = v_raw[c][:, h, :].rearrange("p (r c i) -> p c r i", r=PACK, i=RUN)
+            scalar_round(v_bf[c][:, h, :, :].rearrange("p (c i) r -> p c r i", i=RUN), src)
+
+        def quantize_values(c):
+            quantize(window(v_mx[c], everywhere, 0, HEADS * VALUES), v_bf[c][:].rearrange("p h e r -> p (h e r)"))
+
+        def scale_mask(scaler, c, r, first=0, last=QUERIES):
+            scaler(mask_t[c][:, r, first:last], mask_raw[c][r // 2][:, r % 2, first:last], t_sb[:, c, r : r + 1])
+
+        def exp_scores(c, b, h):
+            rows = slice(ROWS * h, ROWS * (h + 1))
+            bank = score_pool[h].tile([P, PACK, BLOCK], F32, name="scores%d" % h)
+            for r in range(PACK):
+                keys = window(k_mx[c][r // 2], rows, P * (r % 2), P)
+                product(bank[:, r, :], keys, window(q_mx[b], rows, 0, BLOCK), True, True)
+            dst = p_sb[c][h][b // 2][:, PASS * (b % 2) : PASS * (b % 2 + 1)]
+            nc.scalar.activation(
+                out=dst.rearrange("p (c r i) -> p c r i", r=PACK, i=RUN),
+                in_=bank[:].rearrange("p r (c i) -> p c r i", i=RUN),
+                func=ACT.Exp,
+            )
+
+        def weigh(c, h, b, count):
+            cols = slice(PASS * (b % 2), PASS * (b % 2 + count))
+            nc.vector.tensor_tensor(
+                out=w_bf[c][h][b // 2][:, cols].rearrange("p (c i r) -> p c r i", r=PACK, i=RUN),
+                in0=p_sb[c][h][b // 2][:, cols].rearrange("p (c r i) -> p c r i", r=PACK, i=RUN),
+                in1=mask_t[c][:, :, BLOCK * b : BLOCK * (b + count)].rearrange("p r (c i) -> p c r i", i=RUN),
+                op=ALU.mult,
+            )
+
+        def quantize_weights(c, h, b, count):
+            operand = window(w_mx[c][h][b // 2], everywhere, BLOCK * (b % 2), BLOCK * count)
+            quantize(operand, w_bf[c][h][b // 2][:, PASS * (b % 2) : PASS * (b % 2 + count)])
+
+        def second_product(b, h):
+            for c in range(PASSES):
+                weights = window(w_mx[c][h][b // 2], everywhere, BLOCK * (b % 2), BLOCK)
+                product(y[b][:, h, :], weights, window(v_mx[c], everywhere, VALUES * h, VALUES), c == 0, c == PASSES - 1)
+
+        def denominators(b):
+            nc.vector.scalar_tensor_tensor(
+                out=den[b][:], in0=y[b][:, :, VALUES - 1], scalar=2.0, in1=sink2[:, :, b], op0=ALU.mult, op1=ALU.add
+            )
+
+        def gate(b):
+            nc.vector.scalar_tensor_tensor(
+                out=gated[b][:], in0=tanh_og[:, :, b, :], scalar=1.0, in1=y[b][:], op0=ALU.add, op1=ALU.mult
+            )
+
+        def invert(b):
+            nc.vector.reciprocal(out=inv[b][:], in_=den[b][:])
+
+        def finish(b):
+            for h in range(HEADS):
+                scalar_scale(result[b][:, h, :], gated[b][:, h, :], inv[b][:, h : h + 1])
+            nc.sync.dma_start(out=out[:, BLOCK * b : BLOCK * (b + 1), :].rearrange("h p e -> p h e"), in_=result[b][:])
+
+        round_keys(vector_round, 0, 0, 0, 128)
+        round_keys(scalar_round, 0, 1, 0, 128)
+        quantize_keys(0, 0)
+        quantize_keys(0, 1)
+        round_queries(vector_round, 0)
+        round_queries(scalar_round, 1)
+        round_queries(vector_round, 2)
+        round_queries(scalar_round, 3)
+        quantize_queries(0)
+        quantize_queries(1)
+        quantize_queries(2)
+        quantize_queries(3)
+        exp_scores(0, 0, 0)
+        exp_scores(0, 1, 0)
+        exp_scores(0, 0, 1)
+        exp_scores(0, 1, 1)
+        scale_mask(vector_scale, 0, 0, 0, 512)
+        scale_mask(vector_scale, 0, 1, 0, 512)
+        scale_mask(vector_scale, 0, 2, 0, 512)
+        scale_mask(vector_scale, 0, 3, 0, 512)
+        weigh(0, 0, 0, 2)
+        weigh(0, 1, 0, 2)
+        quantize_weights(0, 0, 0, 2)
+        exp_scores(0, 2, 0)
+        exp_scores(0, 3, 0)
+        round_keys(vector_round, 1, 0, 0, 128)
+        round_keys(vector_round, 1, 1, 0, 128)
+        quantize_weights(0, 1, 0, 2)
+        quantize_keys(1, 0)
+        quantize_keys(1, 1)
+        exp_scores(0, 2, 1)
+        exp_scores(0, 3, 1)
+        weigh(0, 0, 2, 2)
+        weigh(0, 1, 2, 2)
+        quantize_weights(0, 0, 2, 2)
+        scale_mask(scalar_scale, 1, 0, 0, 512)
+        scale_mask(scalar_scale, 1, 1, 0, 512)
+        scale_mask(scalar_scale, 1, 2, 0, 512)
+        scale_mask(scalar_scale, 1, 3, 0, 512)
+        quantize_weights(0, 1, 2, 2)
+        exp_scores(1, 0, 0)
+        exp_scores(1, 1, 0)
+        exp_scores(1, 0, 1)
+        exp_scores(1, 1, 1)
+        round_values(0, 0)
+        round_values(0, 1)
+        weigh(1, 0, 0, 2)
+        weigh(1, 1, 0, 2)
+        quantize_weights(1, 0, 0, 2)
+        quantize_values(0)
+        quantize_weights(1, 1, 0, 2)
+        round_values(1, 0)
+        exp_scores(1, 2, 0)
+        round_values(1, 1)
+        exp_scores(1, 2, 1)
+        exp_scores(1, 3, 0)
+        exp_scores(1, 3, 1)
+        scalar_scale(sink2[:], sink_sb[:], 2.0)
+        nc.scalar.activation(out=tanh_og[:], in_=og_sb[:], func=ACT.Tanh, scale=0.5)
+        weigh(1, 0, 2, 1)
+        quantize_values(1)
+        second_product(0, 0)
+        second_product(0, 1)
+        second_product(1, 0)
+        second_product(1, 1)
+        weigh(1, 1, 2, 1)
+        quantize_weights(1, 0, 2, 1)
+        second_product(2, 0)
+        weigh(1, 0, 3, 1)
+        quantize_weights(1, 1, 2, 1)
+        second_product(2, 1)
+        denominators(0)
+        denominators(1)
+        weigh(1, 1, 3, 1)
+        quantize_weights(1, 0, 3, 1)
+        second_product(3, 0)
+        invert(0)
+        invert(1)
+        quantize_weights(1, 1, 3, 1)
+        second_product(3, 1)
+        gate(0)
+        denominators(2)
+        finish(0)
+        gate(1)
+        invert(2)
+        finish(1)
+        denominators(3)
+        gate(2)
+        invert(3)
+        finish(2)
+        gate(3)
+        finish(3)

@@ -20,7 +20,7 @@ PASS = P * PACK
 PASSES = TOKENS // PASS
 BLOCK = 128
 BLOCKS = QUERIES // BLOCK
-RUN = 2
+RUN = 4
 
 
 def tile_rows_a_exp_mask_sink_gate_kernel(tc, qT, kT, t, v, mask, sink, og, out):
@@ -28,7 +28,7 @@ def tile_rows_a_exp_mask_sink_gate_kernel(tc, qT, kT, t, v, mask, sink, og, out)
     with ExitStack() as ctx:
         sbuf = ctx.enter_context(tc.tile_pool(name="sbuf", bufs=1))
         score_pool = [ctx.enter_context(tc.psum_pool(name="scores%d" % h, bufs=2)) for h in range(HEADS)]
-        y_pool = ctx.enter_context(tc.psum_pool(name="y", bufs=1))
+        y_pool = ctx.enter_context(tc.psum_pool(name="y", bufs=4))
         ctx.enter_context(nc.allow_non_contiguous_dma(reason="one sink a partition and head"))
         ctx.enter_context(tc.manual_schedule())
 
@@ -100,17 +100,18 @@ def tile_rows_a_exp_mask_sink_gate_kernel(tc, qT, kT, t, v, mask, sink, og, out)
         q_mx = mx_tiles("q", BLOCKS, BLOCK)
         v_bf = tiles("v_bf", PASSES, [P, HEADS, VALUES, PACK], BF16)
         v_mx = mx_tiles("v", PASSES, HEADS * VALUES)
-        mask_t = tiles("mask_t", PASSES, [P, PACK, QUERIES], F32)
-        p_sb = [[tiles("p%d%d_" % (c, h), 2, [P, 2 * PASS], F32) for h in range(HEADS)] for c in range(PASSES)]
-        w_bf = [[tiles("w%d%d_" % (c, h), 2, [P, 2 * PASS], BF16) for h in range(HEADS)] for c in range(PASSES)]
-        w_mx = [[mx_tiles("w%d%d_" % (c, h), 2, 2 * BLOCK) for h in range(HEADS)] for c in range(PASSES)]
+        mask_t = tiles("mask_t", PASSES, [P, QUERIES // RUN, PACK, RUN], F32)
+        p_sb = [tiles("p%d_" % c, BLOCKS, [P, HEADS, PASS], F32) for c in range(PASSES)]
+        w_bf = [tiles("w%d_" % c, BLOCKS, [P, HEADS, PASS], BF16) for c in range(PASSES)]
+        w_mx = [mx_tiles("w%d_" % c, BLOCKS, HEADS * BLOCK) for c in range(PASSES)]
         tanh_og = tiles("tanh_og", 1, [P, HEADS, BLOCKS, VALUES], F32)[0]
         sink2 = tiles("sink2_", 1, [P, HEADS, BLOCKS], F32)[0]
         den = tiles("den", BLOCKS, [P, HEADS], F32)
         inv = tiles("inv", BLOCKS, [P, HEADS], F32)
         gated = tiles("gated", BLOCKS, [P, HEADS, VALUES], F32)
         result = tiles("result", BLOCKS, [P, HEADS, VALUES], F32)
-        y = [y_pool.tile([P, HEADS, VALUES], F32, name="y%d" % b) for b in range(BLOCKS)]
+        y = {}
+        banks = {}
 
         def round_keys(rounder, c, pair, first, last):
             src = k_raw[c][:, :, PACK * first : PACK * last].rearrange("p j (s r) -> p s j r", r=PACK)
@@ -134,37 +135,46 @@ def tile_rows_a_exp_mask_sink_gate_kernel(tc, qT, kT, t, v, mask, sink, og, out)
             quantize(window(v_mx[c], everywhere, 0, HEADS * VALUES), v_bf[c][:].rearrange("p h e r -> p (h e r)"))
 
         def scale_mask(scaler, c, r, first=0, last=QUERIES):
-            scaler(mask_t[c][:, r, first:last], mask_raw[c][r // 2][:, r % 2, first:last], t_sb[:, c, r : r + 1])
+            src = mask_raw[c][r // 2][:, r % 2, first:last].rearrange("p (c i) -> p c i", i=RUN)
+            scaler(mask_t[c][:, first // RUN : last // RUN, r, :], src, t_sb[:, c, r : r + 1])
+
+        def scores(c, b):
+            for h in range(HEADS):
+                banks[c, b, h] = score_pool[h].tile([P, PACK, BLOCK], F32, name="scores%d" % h)
+            for r in range(PACK):
+                for h in range(HEADS):
+                    rows = slice(ROWS * h, ROWS * (h + 1))
+                    keys = window(k_mx[c][r // 2], rows, P * (r % 2), P)
+                    product(banks[c, b, h][:, r, :], keys, window(q_mx[b], rows, 0, BLOCK), True, True)
 
         def exp_scores(c, b, h):
-            rows = slice(ROWS * h, ROWS * (h + 1))
-            bank = score_pool[h].tile([P, PACK, BLOCK], F32, name="scores%d" % h)
-            for r in range(PACK):
-                keys = window(k_mx[c][r // 2], rows, P * (r % 2), P)
-                product(bank[:, r, :], keys, window(q_mx[b], rows, 0, BLOCK), True, True)
-            dst = p_sb[c][h][b // 2][:, PASS * (b % 2) : PASS * (b % 2 + 1)]
+            if h == 0:
+                scores(c, b)
             nc.scalar.activation(
-                out=dst.rearrange("p (c r i) -> p c r i", r=PACK, i=RUN),
-                in_=bank[:].rearrange("p r (c i) -> p c r i", i=RUN),
+                out=p_sb[c][b][:, h, :].rearrange("p (c r i) -> p c r i", r=PACK, i=RUN),
+                in_=banks[c, b, h][:].rearrange("p r (c i) -> p c r i", i=RUN),
                 func=ACT.Exp,
             )
 
         def weigh(c, h, b, count):
-            cols = slice(PASS * (b % 2), PASS * (b % 2 + count))
+            heads = slice(h, h + count)
+            factors = mask_t[c][:, BLOCK * b // RUN : BLOCK * (b + 1) // RUN, :, :].rearrange("p c r i -> p (c r i)")
             nc.vector.tensor_tensor(
-                out=w_bf[c][h][b // 2][:, cols].rearrange("p (c i r) -> p c r i", r=PACK, i=RUN),
-                in0=p_sb[c][h][b // 2][:, cols].rearrange("p (c r i) -> p c r i", r=PACK, i=RUN),
-                in1=mask_t[c][:, :, BLOCK * b : BLOCK * (b + count)].rearrange("p r (c i) -> p c r i", i=RUN),
+                out=w_bf[c][b][:, heads, :].rearrange("p h (c i r) -> p (h c) r i", r=PACK, i=RUN),
+                in0=p_sb[c][b][:, heads, :],
+                in1=factors.unsqueeze(1).to_broadcast([P, count, PASS]),
                 op=ALU.mult,
             )
 
         def quantize_weights(c, h, b, count):
-            operand = window(w_mx[c][h][b // 2], everywhere, BLOCK * (b % 2), BLOCK * count)
-            quantize(operand, w_bf[c][h][b // 2][:, PASS * (b % 2) : PASS * (b % 2 + count)])
+            operand = window(w_mx[c][b], everywhere, BLOCK * h, BLOCK * count)
+            quantize(operand, w_bf[c][b][:, h : h + count, :].rearrange("p h n -> p (h n)"))
 
         def second_product(b, h):
+            if h == 0:
+                y[b] = y_pool.tile([P, HEADS, VALUES], F32, name="y")
             for c in range(PASSES):
-                weights = window(w_mx[c][h][b // 2], everywhere, BLOCK * (b % 2), BLOCK)
+                weights = window(w_mx[c][b], everywhere, BLOCK * h, BLOCK)
                 product(y[b][:, h, :], weights, window(v_mx[c], everywhere, VALUES * h, VALUES), c == 0, c == PASSES - 1)
 
         def denominators(b):
@@ -198,50 +208,50 @@ def tile_rows_a_exp_mask_sink_gate_kernel(tc, qT, kT, t, v, mask, sink, og, out)
         quantize_queries(2)
         quantize_queries(3)
         exp_scores(0, 0, 0)
-        exp_scores(0, 1, 0)
         exp_scores(0, 0, 1)
-        exp_scores(0, 1, 1)
         scale_mask(vector_scale, 0, 0, 0, 512)
         scale_mask(vector_scale, 0, 1, 0, 512)
         scale_mask(vector_scale, 0, 2, 0, 512)
         scale_mask(vector_scale, 0, 3, 0, 512)
+        exp_scores(0, 1, 0)
+        exp_scores(0, 1, 1)
         weigh(0, 0, 0, 2)
-        weigh(0, 1, 0, 2)
-        quantize_weights(0, 0, 0, 2)
         exp_scores(0, 2, 0)
-        exp_scores(0, 3, 0)
-        round_keys(vector_round, 1, 0, 0, 128)
-        round_keys(vector_round, 1, 1, 0, 128)
-        quantize_weights(0, 1, 0, 2)
-        quantize_keys(1, 0)
-        quantize_keys(1, 1)
         exp_scores(0, 2, 1)
+        weigh(0, 0, 1, 2)
+        round_keys(scalar_round, 1, 1, 0, 128)
+        round_keys(vector_round, 1, 0, 0, 128)
+        quantize_keys(1, 0)
+        quantize_weights(0, 0, 0, 2)
+        quantize_weights(0, 0, 1, 2)
+        quantize_keys(1, 1)
+        exp_scores(0, 3, 0)
         exp_scores(0, 3, 1)
-        weigh(0, 0, 2, 2)
-        weigh(0, 1, 2, 2)
-        quantize_weights(0, 0, 2, 2)
         scale_mask(scalar_scale, 1, 0, 0, 512)
-        scale_mask(scalar_scale, 1, 1, 0, 512)
-        scale_mask(scalar_scale, 1, 2, 0, 512)
-        scale_mask(scalar_scale, 1, 3, 0, 512)
-        quantize_weights(0, 1, 2, 2)
+        weigh(0, 0, 2, 2)
+        scale_mask(vector_scale, 1, 1, 0, 512)
+        scale_mask(vector_scale, 1, 2, 0, 512)
+        scale_mask(vector_scale, 1, 3, 0, 512)
         exp_scores(1, 0, 0)
-        exp_scores(1, 1, 0)
         exp_scores(1, 0, 1)
-        exp_scores(1, 1, 1)
+        weigh(0, 0, 3, 2)
+        quantize_weights(0, 0, 2, 2)
         round_values(0, 0)
+        exp_scores(1, 1, 0)
+        exp_scores(1, 1, 1)
         round_values(0, 1)
         weigh(1, 0, 0, 2)
-        weigh(1, 1, 0, 2)
-        quantize_weights(1, 0, 0, 2)
-        quantize_values(0)
-        quantize_weights(1, 1, 0, 2)
+        quantize_weights(0, 0, 3, 2)
         round_values(1, 0)
         exp_scores(1, 2, 0)
-        round_values(1, 1)
         exp_scores(1, 2, 1)
+        round_values(1, 1)
+        weigh(1, 0, 1, 2)
+        quantize_weights(1, 0, 0, 2)
+        quantize_values(0)
         exp_scores(1, 3, 0)
         exp_scores(1, 3, 1)
+        quantize_weights(1, 0, 1, 2)
         scalar_scale(sink2[:], sink_sb[:], 2.0)
         nc.scalar.activation(out=tanh_og[:], in_=og_sb[:], func=ACT.Tanh, scale=0.5)
         weigh(1, 0, 2, 1)

@@ -20,7 +20,7 @@ PASS = P * PACK
 PASSES = TOKENS // PASS
 BLOCK = 128
 BLOCKS = QUERIES // BLOCK
-RUN = 4
+RUN = 2
 
 
 def tile_rows_a_exp_mask_sink_gate_kernel(tc, qT, kT, t, v, mask, sink, og, out):
@@ -28,7 +28,7 @@ def tile_rows_a_exp_mask_sink_gate_kernel(tc, qT, kT, t, v, mask, sink, og, out)
     with ExitStack() as ctx:
         sbuf = ctx.enter_context(tc.tile_pool(name="sbuf", bufs=1))
         score_pool = [ctx.enter_context(tc.psum_pool(name="scores%d" % h, bufs=2)) for h in range(HEADS)]
-        y_pool = ctx.enter_context(tc.psum_pool(name="y", bufs=4))
+        y_pool = ctx.enter_context(tc.psum_pool(name="y", bufs=1))
         ctx.enter_context(nc.allow_non_contiguous_dma(reason="one sink a partition and head"))
         ctx.enter_context(tc.manual_schedule())
 
@@ -100,18 +100,17 @@ def tile_rows_a_exp_mask_sink_gate_kernel(tc, qT, kT, t, v, mask, sink, og, out)
         q_mx = mx_tiles("q", BLOCKS, BLOCK)
         v_bf = tiles("v_bf", PASSES, [P, HEADS, VALUES, PACK], BF16)
         v_mx = mx_tiles("v", PASSES, HEADS * VALUES)
-        mask_t = tiles("mask_t", PASSES, [P, QUERIES // RUN, PACK, RUN], F32)
-        p_sb = [tiles("p%d_" % c, BLOCKS, [P, HEADS, PASS], F32) for c in range(PASSES)]
-        w_bf = [tiles("w%d_" % c, BLOCKS, [P, HEADS, PASS], BF16) for c in range(PASSES)]
-        w_mx = [mx_tiles("w%d_" % c, BLOCKS, HEADS * BLOCK) for c in range(PASSES)]
+        mask_t = tiles("mask_t", PASSES, [P, PACK, QUERIES], F32)
+        p_sb = [[tiles("p%d%d_" % (c, h), 2, [P, 2 * PASS], F32) for h in range(HEADS)] for c in range(PASSES)]
+        w_bf = [[tiles("w%d%d_" % (c, h), 2, [P, 2 * PASS], BF16) for h in range(HEADS)] for c in range(PASSES)]
+        w_mx = [[mx_tiles("w%d%d_" % (c, h), 2, 2 * BLOCK) for h in range(HEADS)] for c in range(PASSES)]
         tanh_og = tiles("tanh_og", 1, [P, HEADS, BLOCKS, VALUES], F32)[0]
-        sink2 = tiles("sink2_", 1, [P, HEADS, BLOCKS], F32)[0]
+        gate_sb = tiles("gate", 1, [P, HEADS, BLOCKS, VALUES], F32)[0]
         den = tiles("den", BLOCKS, [P, HEADS], F32)
         inv = tiles("inv", BLOCKS, [P, HEADS], F32)
-        gated = tiles("gated", BLOCKS, [P, HEADS, VALUES], F32)
-        result = tiles("result", BLOCKS, [P, HEADS, VALUES], F32)
-        y = {}
         banks = {}
+        result = tiles("result", BLOCKS, [P, HEADS, VALUES], F32)
+        y = [y_pool.tile([P, HEADS, VALUES], F32, name="y%d" % b) for b in range(BLOCKS)]
 
         def round_keys(rounder, c, pair, first, last):
             src = k_raw[c][:, :, PACK * first : PACK * last].rearrange("p j (s r) -> p s j r", r=PACK)
@@ -135,8 +134,7 @@ def tile_rows_a_exp_mask_sink_gate_kernel(tc, qT, kT, t, v, mask, sink, og, out)
             quantize(window(v_mx[c], everywhere, 0, HEADS * VALUES), v_bf[c][:].rearrange("p h e r -> p (h e r)"))
 
         def scale_mask(scaler, c, r, first=0, last=QUERIES):
-            src = mask_raw[c][r // 2][:, r % 2, first:last].rearrange("p (c i) -> p c i", i=RUN)
-            scaler(mask_t[c][:, first // RUN : last // RUN, r, :], src, t_sb[:, c, r : r + 1])
+            scaler(mask_t[c][:, r, first:last], mask_raw[c][r // 2][:, r % 2, first:last], t_sb[:, c, r : r + 1])
 
         def scores(c, b):
             for h in range(HEADS):
@@ -150,49 +148,55 @@ def tile_rows_a_exp_mask_sink_gate_kernel(tc, qT, kT, t, v, mask, sink, og, out)
         def exp_scores(c, b, h):
             if h == 0:
                 scores(c, b)
+            dst = p_sb[c][h][b // 2][:, PASS * (b % 2) : PASS * (b % 2 + 1)]
             nc.scalar.activation(
-                out=p_sb[c][b][:, h, :].rearrange("p (c r i) -> p c r i", r=PACK, i=RUN),
+                out=dst.rearrange("p (c r i) -> p c r i", r=PACK, i=RUN),
                 in_=banks[c, b, h][:].rearrange("p r (c i) -> p c r i", i=RUN),
                 func=ACT.Exp,
             )
 
         def weigh(c, h, b, count):
-            heads = slice(h, h + count)
-            factors = mask_t[c][:, BLOCK * b // RUN : BLOCK * (b + 1) // RUN, :, :].rearrange("p c r i -> p (c r i)")
+            cols = slice(PASS * (b % 2), PASS * (b % 2 + count))
             nc.vector.tensor_tensor(
-                out=w_bf[c][b][:, heads, :].rearrange("p h (c i r) -> p (h c) r i", r=PACK, i=RUN),
-                in0=p_sb[c][b][:, heads, :],
-                in1=factors.unsqueeze(1).to_broadcast([P, count, PASS]),
+                out=w_bf[c][h][b // 2][:, cols].rearrange("p (c i r) -> p c r i", r=PACK, i=RUN),
+                in0=p_sb[c][h][b // 2][:, cols].rearrange("p (c r i) -> p c r i", r=PACK, i=RUN),
+                in1=mask_t[c][:, :, BLOCK * b : BLOCK * (b + count)].rearrange("p r (c i) -> p c r i", i=RUN),
                 op=ALU.mult,
             )
 
         def quantize_weights(c, h, b, count):
-            operand = window(w_mx[c][b], everywhere, BLOCK * h, BLOCK * count)
-            quantize(operand, w_bf[c][b][:, h : h + count, :].rearrange("p h n -> p (h n)"))
+            operand = window(w_mx[c][h][b // 2], everywhere, BLOCK * (b % 2), BLOCK * count)
+            quantize(operand, w_bf[c][h][b // 2][:, PASS * (b % 2) : PASS * (b % 2 + count)])
 
         def second_product(b, h):
-            if h == 0:
-                y[b] = y_pool.tile([P, HEADS, VALUES], F32, name="y")
             for c in range(PASSES):
-                weights = window(w_mx[c][b], everywhere, BLOCK * h, BLOCK)
+                weights = window(w_mx[c][h][b // 2], everywhere, BLOCK * (b % 2), BLOCK)
                 product(y[b][:, h, :], weights, window(v_mx[c], everywhere, VALUES * h, VALUES), c == 0, c == PASSES - 1)
 
         def denominators(b):
-            nc.vector.scalar_tensor_tensor(
-                out=den[b][:], in0=y[b][:, :, VALUES - 1], scalar=2.0, in1=sink2[:, :, b], op0=ALU.mult, op1=ALU.add
-            )
-
-        def gate(b):
-            nc.vector.scalar_tensor_tensor(
-                out=gated[b][:], in0=tanh_og[:, :, b, :], scalar=1.0, in1=y[b][:], op0=ALU.add, op1=ALU.mult
-            )
+            nc.vector.tensor_tensor(out=den[b][:], in0=y[b][:, :, VALUES - 1], in1=sink_sb[:, :, b], op=ALU.add)
 
         def invert(b):
             nc.vector.reciprocal(out=inv[b][:], in_=den[b][:])
 
+        def sigmoid_gate(first, last):
+            blocks = slice(first, last)
+            nc.scalar.activation(out=tanh_og[:, :, blocks, :], in_=og_sb[:, :, blocks, :], func=ACT.Tanh, scale=0.5)
+
+        def affine_gate(first, last):
+            blocks = slice(first, last)
+            nc.scalar.activation(out=gate_sb[:, :, blocks, :], in_=tanh_og[:, :, blocks, :], func=ACT.Copy, scale=0.5, bias=0.5)
+
         def finish(b):
             for h in range(HEADS):
-                scalar_scale(result[b][:, h, :], gated[b][:, h, :], inv[b][:, h : h + 1])
+                nc.vector.scalar_tensor_tensor(
+                    out=result[b][:, h, :],
+                    in0=y[b][:, h, :],
+                    scalar=inv[b][:, h : h + 1],
+                    in1=gate_sb[:, h, b, :],
+                    op0=ALU.mult,
+                    op1=ALU.mult,
+                )
             nc.sync.dma_start(out=out[:, BLOCK * b : BLOCK * (b + 1), :].rearrange("h p e -> p h e"), in_=result[b][:])
 
         round_keys(vector_round, 0, 0, 0, 128)
@@ -215,45 +219,49 @@ def tile_rows_a_exp_mask_sink_gate_kernel(tc, qT, kT, t, v, mask, sink, og, out)
         scale_mask(vector_scale, 0, 3, 0, 512)
         exp_scores(0, 1, 0)
         exp_scores(0, 1, 1)
-        weigh(0, 0, 0, 2)
+        weigh(0, 0, 0, 1)
+        weigh(0, 1, 0, 1)
         exp_scores(0, 2, 0)
         exp_scores(0, 2, 1)
-        weigh(0, 0, 1, 2)
+        weigh(0, 0, 1, 1)
         round_keys(scalar_round, 1, 1, 0, 128)
         round_keys(vector_round, 1, 0, 0, 128)
+        weigh(0, 1, 1, 1)
         quantize_keys(1, 0)
         quantize_weights(0, 0, 0, 2)
-        quantize_weights(0, 0, 1, 2)
+        quantize_weights(0, 1, 0, 2)
+        scale_mask(vector_scale, 1, 1, 0, 512)
         quantize_keys(1, 1)
         exp_scores(0, 3, 0)
         exp_scores(0, 3, 1)
         scale_mask(scalar_scale, 1, 0, 0, 512)
-        weigh(0, 0, 2, 2)
-        scale_mask(vector_scale, 1, 1, 0, 512)
         scale_mask(vector_scale, 1, 2, 0, 512)
         scale_mask(vector_scale, 1, 3, 0, 512)
+        weigh(0, 0, 2, 2)
         exp_scores(1, 0, 0)
         exp_scores(1, 0, 1)
-        weigh(0, 0, 3, 2)
-        quantize_weights(0, 0, 2, 2)
-        round_values(0, 0)
         exp_scores(1, 1, 0)
         exp_scores(1, 1, 1)
+        weigh(0, 1, 2, 2)
+        quantize_weights(0, 0, 2, 2)
+        round_values(0, 0)
         round_values(0, 1)
         weigh(1, 0, 0, 2)
-        quantize_weights(0, 0, 3, 2)
+        quantize_weights(0, 1, 2, 2)
         round_values(1, 0)
         exp_scores(1, 2, 0)
         exp_scores(1, 2, 1)
         round_values(1, 1)
-        weigh(1, 0, 1, 2)
+        weigh(1, 1, 0, 2)
         quantize_weights(1, 0, 0, 2)
         quantize_values(0)
         exp_scores(1, 3, 0)
         exp_scores(1, 3, 1)
-        quantize_weights(1, 0, 1, 2)
-        scalar_scale(sink2[:], sink_sb[:], 2.0)
-        nc.scalar.activation(out=tanh_og[:], in_=og_sb[:], func=ACT.Tanh, scale=0.5)
+        quantize_weights(1, 1, 0, 2)
+        sigmoid_gate(0, 2)
+        sigmoid_gate(2, 4)
+        affine_gate(0, 2)
+        affine_gate(2, 4)
         weigh(1, 0, 2, 1)
         quantize_values(1)
         second_product(0, 0)
@@ -273,17 +281,13 @@ def tile_rows_a_exp_mask_sink_gate_kernel(tc, qT, kT, t, v, mask, sink, og, out)
         second_product(3, 0)
         invert(0)
         invert(1)
+        denominators(2)
         quantize_weights(1, 1, 3, 1)
         second_product(3, 1)
-        gate(0)
-        denominators(2)
-        finish(0)
-        gate(1)
         invert(2)
-        finish(1)
+        finish(0)
         denominators(3)
-        gate(2)
+        finish(1)
         invert(3)
         finish(2)
-        gate(3)
         finish(3)

@@ -29,22 +29,26 @@ def tile_rows_a_exp_mask_sink_gate_kernel(tc, qT, kT, t, v, mask, sink, og, out)
         sbuf = ctx.enter_context(tc.tile_pool(name="sbuf", bufs=1))
         score_pool = [ctx.enter_context(tc.psum_pool(name="scores%d" % h, bufs=2)) for h in range(HEADS)]
         y_pool = ctx.enter_context(tc.psum_pool(name="y", bufs=1))
-        ctx.enter_context(nc.allow_non_contiguous_dma(reason="one sink a partition and head"))
+        ctx.enter_context(nc.allow_non_contiguous_dma(reason="one sink for each partition, head and block"))
         ctx.enter_context(tc.manual_schedule())
 
         def tiles(name, count, shape, dtype):
-            return [sbuf.tile(shape, dtype, name="%s%d" % (name, i), align_bytes=64) for i in range(count)]
+            return [sbuf.tile(shape, dtype, name="%s%d" % (name, n), align_bytes=64) for n in range(count)]
 
         def mx_tiles(name, count, words):
-            return list(zip(tiles(name + "_codes", count, [P, words], U32), tiles(name + "_scales", count, [P, words], U8)))
+            codes = tiles(name + "_codes", count, [P, words], U32)
+            scales = tiles(name + "_scales", count, [P, words], U8)
+            return list(zip(codes, scales))
+
+        def window(operand, rows, first, count):
+            return operand[0][rows, first : first + count], operand[1][rows, first : first + count]
 
         def quantize(operand, source):
-            codes, scales = operand
-            nc.vector.quantize_mx(out=codes.bitcast(FP8X4), scales=scales, in_=source)
+            nc.vector.quantize_mx(out=operand[0].bitcast(FP8X4), scales=operand[1], in_=source)
 
-        def product(result, stationary, moving, start, stop):
+        def product(dst, stationary, moving, start, stop):
             nc.tensor.matmul_mx(
-                out=result,
+                out=dst,
                 lhsT=stationary[0].bitcast(FP8X4),
                 lhsT_scale=stationary[1],
                 rhs=moving[0].bitcast(FP8X4),
@@ -52,9 +56,6 @@ def tile_rows_a_exp_mask_sink_gate_kernel(tc, qT, kT, t, v, mask, sink, og, out)
                 start=start,
                 stop=stop,
             )
-
-        def window(operand, rows, first, count):
-            return operand[0][rows, first : first + count], operand[1][rows, first : first + count]
 
         def vector_round(dst, src):
             nc.vector.tensor_copy(out=dst, in_=src)
@@ -72,27 +73,29 @@ def tile_rows_a_exp_mask_sink_gate_kernel(tc, qT, kT, t, v, mask, sink, og, out)
         t_sb = tiles("t", 1, [P, PASSES, PACK], F32)[0]
         q_raw = tiles("q_raw", 1, [P, PACK, QUERIES], F32)[0]
         k_raw = tiles("k_raw", PASSES, [P, PACK, PASS], F32)
-        mask_raw = [tiles("mask_raw%d_" % c, 2, [P, 2, QUERIES], F32) for c in range(PASSES)]
+        mask_early = tiles("mask_early", PASSES, [P, PACK - 1, QUERIES], F32)
+        mask_late = tiles("mask_late", PASSES, [P, QUERIES], F32)
         v_raw = tiles("v_raw", PASSES, [P, HEADS, PACK * VALUES], F32)
         og_sb = tiles("og", 1, [P, HEADS, BLOCKS, VALUES], F32)[0]
         sink_sb = tiles("sink", 1, [P, HEADS, BLOCKS], F32)[0]
 
         q_rows = qT.rearrange("h (p j) q -> (h p) j q", j=PACK)
         k_rows = kT.rearrange("h (p j) n -> (h p) j n", j=PACK)
-        nc.scalar.dma_start(out=t_sb[:], in_=t.rearrange("(c p r) o -> p c (r o)", c=PASSES, r=PACK))
+        mask_rows = mask.rearrange("(c s r) q -> c s r q", c=PASSES, r=PACK)
+        v_rows = v.rearrange("h (c s r) e -> c s h (r e)", c=PASSES, r=PACK)
+        nc.scalar.dma_start(out=t_sb[:], in_=t.rearrange("(c s r) o -> s c (r o)", c=PASSES, r=PACK))
         for c in range(PASSES):
-            tokens = slice(PASS * c, PASS * (c + 1))
-            nc.sync.dma_start(out=k_raw[c][:], in_=k_rows[:, :, tokens])
+            nc.sync.dma_start(out=k_raw[c][:], in_=k_rows[:, :, PASS * c : PASS * (c + 1)])
             if c == 0:
                 nc.sync.dma_start(out=q_raw[:], in_=q_rows)
-            mask_rows = mask[tokens, :].rearrange("(p r) q -> p r q", r=PACK)
-            for pair in range(2):
-                nc.sync.dma_start(out=mask_raw[c][pair][:], in_=mask_rows[:, 2 * pair : 2 * pair + 2, :])
+            nc.sync.dma_start(out=mask_early[c][:], in_=mask_rows[c][:, 0 : PACK - 1, :])
+            nc.sync.dma_start(out=mask_late[c][:], in_=mask_rows[c][:, PACK - 1, :])
         for c in range(PASSES):
-            tokens = slice(PASS * c, PASS * (c + 1))
-            nc.sync.dma_start(out=v_raw[c][:], in_=v[:, tokens, :].rearrange("h (p r) e -> p h (r e)", r=PACK))
-        nc.sync.dma_start(out=og_sb[:].rearrange("p h b e -> p (h b) e"), in_=og.rearrange("h (b p) e -> p (h b) e", p=P))
-        nc.sync.dma_start(out=sink_sb[:], in_=sink.rearrange("h (b p) o -> p h (b o)", p=P))
+            nc.sync.dma_start(out=v_raw[c][:], in_=v_rows[c])
+        nc.sync.dma_start(
+            out=og_sb[:].rearrange("m h b e -> m (h b) e"), in_=og.rearrange("h (b m) e -> m (h b) e", m=BLOCK)
+        )
+        nc.sync.dma_start(out=sink_sb[:], in_=sink.rearrange("h (b m) o -> m h (b o)", m=BLOCK))
 
         k_bf = [tiles("k_bf%d_" % c, 2, [P, 2, P, PACK], BF16) for c in range(PASSES)]
         k_mx = [mx_tiles("k%d_" % c, 2, 2 * P) for c in range(PASSES)]
@@ -105,62 +108,58 @@ def tile_rows_a_exp_mask_sink_gate_kernel(tc, qT, kT, t, v, mask, sink, og, out)
         w_bf = [[tiles("w%d%d_" % (c, h), 2, [P, 2 * PASS], BF16) for h in range(HEADS)] for c in range(PASSES)]
         w_mx = [[mx_tiles("w%d%d_" % (c, h), 2, 2 * BLOCK) for h in range(HEADS)] for c in range(PASSES)]
         tanh_og = tiles("tanh_og", 1, [P, HEADS, BLOCKS, VALUES], F32)[0]
-        gate_sb = tiles("gate", 1, [P, HEADS, BLOCKS, VALUES], F32)[0]
+        gate = tiles("gate", 1, [P, HEADS, BLOCKS, VALUES], F32)[0]
         den = tiles("den", BLOCKS, [P, HEADS], F32)
         inv = tiles("inv", BLOCKS, [P, HEADS], F32)
-        banks = {}
         result = tiles("result", BLOCKS, [P, HEADS, VALUES], F32)
         y = [y_pool.tile([P, HEADS, VALUES], F32, name="y%d" % b) for b in range(BLOCKS)]
 
-        def round_keys(rounder, c, pair, first, last):
-            src = k_raw[c][:, :, PACK * first : PACK * last].rearrange("p j (s r) -> p s j r", r=PACK)
-            rounder(k_bf[c][pair][:, :, first:last, :].rearrange("p r s j -> p s j r"), src[:, :, :, 2 * pair : 2 * pair + 2])
+        def round_keys(rounder, c, pair):
+            src = k_raw[c][:].rearrange("p j (s r) -> p s j r", r=PACK)[:, :, :, 2 * pair : 2 * pair + 2]
+            rounder(k_bf[c][pair][:].rearrange("p r s j -> p s j r"), src)
 
         def quantize_keys(c, pair):
             quantize(window(k_mx[c][pair], everywhere, 0, 2 * P), k_bf[c][pair][:].rearrange("p r s j -> p (r s j)"))
 
         def round_queries(rounder, b):
-            src = q_raw[:, :, BLOCK * b : BLOCK * (b + 1)].rearrange("p j (c i) -> p c j i", i=RUN)
-            rounder(q_bf[b][:].rearrange("p (c i) j -> p c j i", i=RUN), src)
+            src = q_raw[:, :, BLOCK * b : BLOCK * (b + 1)].rearrange("p j (n i) -> p n j i", i=RUN)
+            rounder(q_bf[b][:].rearrange("p (n i) j -> p n j i", i=RUN), src)
 
         def quantize_queries(b):
             quantize(window(q_mx[b], everywhere, 0, BLOCK), q_bf[b][:].rearrange("p q j -> p (q j)"))
 
-        def round_values(c, h):
-            src = v_raw[c][:, h, :].rearrange("p (r c i) -> p c r i", r=PACK, i=RUN)
-            scalar_round(v_bf[c][:, h, :, :].rearrange("p (c i) r -> p c r i", i=RUN), src)
+        def round_values(c):
+            src = v_raw[c][:].rearrange("s h (r n i) -> s h n r i", r=PACK, i=RUN)
+            nc.scalar.copy(out=v_bf[c][:].rearrange("s h (n i) r -> s h n r i", i=RUN), in_=src)
 
         def quantize_values(c):
-            quantize(window(v_mx[c], everywhere, 0, HEADS * VALUES), v_bf[c][:].rearrange("p h e r -> p (h e r)"))
+            quantize(window(v_mx[c], everywhere, 0, HEADS * VALUES), v_bf[c][:].rearrange("s h e r -> s (h e r)"))
 
-        def scale_mask(scaler, c, r, first=0, last=QUERIES):
-            scaler(mask_t[c][:, r, first:last], mask_raw[c][r // 2][:, r % 2, first:last], t_sb[:, c, r : r + 1])
+        def scale_mask(scaler, c, r):
+            src = mask_early[c][:, r, :] if r < PACK - 1 else mask_late[c][:]
+            scaler(mask_t[c][:, r, :], src, t_sb[:, c, r : r + 1])
 
-        def scores(c, b):
-            for h in range(HEADS):
-                banks[c, b, h] = score_pool[h].tile([P, PACK, BLOCK], F32, name="scores%d" % h)
+        def exp_scores(c, b):
+            banks = [score_pool[h].tile([P, PACK, BLOCK], F32, name="scores%d" % h) for h in range(HEADS)]
             for r in range(PACK):
                 for h in range(HEADS):
                     rows = slice(ROWS * h, ROWS * (h + 1))
                     keys = window(k_mx[c][r // 2], rows, P * (r % 2), P)
-                    product(banks[c, b, h][:, r, :], keys, window(q_mx[b], rows, 0, BLOCK), True, True)
-
-        def exp_scores(c, b, h):
-            if h == 0:
-                scores(c, b)
-            dst = p_sb[c][h][b // 2][:, PASS * (b % 2) : PASS * (b % 2 + 1)]
-            nc.scalar.activation(
-                out=dst.rearrange("p (c r i) -> p c r i", r=PACK, i=RUN),
-                in_=banks[c, b, h][:].rearrange("p r (c i) -> p c r i", i=RUN),
-                func=ACT.Exp,
-            )
+                    product(banks[h][:, r, :], keys, window(q_mx[b], rows, 0, BLOCK), True, True)
+            for h in range(HEADS):
+                dst = p_sb[c][h][b // 2][:, PASS * (b % 2) : PASS * (b % 2 + 1)]
+                nc.scalar.activation(
+                    out=dst.rearrange("s (n r i) -> s n r i", r=PACK, i=RUN),
+                    in_=banks[h][:].rearrange("s r (n i) -> s n r i", i=RUN),
+                    func=ACT.Exp,
+                )
 
         def weigh(c, h, b, count):
             cols = slice(PASS * (b % 2), PASS * (b % 2 + count))
             nc.vector.tensor_tensor(
-                out=w_bf[c][h][b // 2][:, cols].rearrange("p (c i r) -> p c r i", r=PACK, i=RUN),
-                in0=p_sb[c][h][b // 2][:, cols].rearrange("p (c r i) -> p c r i", r=PACK, i=RUN),
-                in1=mask_t[c][:, :, BLOCK * b : BLOCK * (b + count)].rearrange("p r (c i) -> p c r i", i=RUN),
+                out=w_bf[c][h][b // 2][:, cols].rearrange("s (n i r) -> s n r i", r=PACK, i=RUN),
+                in0=p_sb[c][h][b // 2][:, cols].rearrange("s (n r i) -> s n r i", r=PACK, i=RUN),
+                in1=mask_t[c][:, :, BLOCK * b : BLOCK * (b + count)].rearrange("s r (n i) -> s n r i", i=RUN),
                 op=ALU.mult,
             )
 
@@ -171,7 +170,8 @@ def tile_rows_a_exp_mask_sink_gate_kernel(tc, qT, kT, t, v, mask, sink, og, out)
         def second_product(b, h):
             for c in range(PASSES):
                 weights = window(w_mx[c][h][b // 2], everywhere, BLOCK * (b % 2), BLOCK)
-                product(y[b][:, h, :], weights, window(v_mx[c], everywhere, VALUES * h, VALUES), c == 0, c == PASSES - 1)
+                values = window(v_mx[c], everywhere, VALUES * h, VALUES)
+                product(y[b][:, h, :], weights, values, c == 0, c == PASSES - 1)
 
         def denominators(b):
             nc.vector.tensor_tensor(out=den[b][:], in0=y[b][:, :, VALUES - 1], in1=sink_sb[:, :, b], op=ALU.add)
@@ -179,95 +179,77 @@ def tile_rows_a_exp_mask_sink_gate_kernel(tc, qT, kT, t, v, mask, sink, og, out)
         def invert(b):
             nc.vector.reciprocal(out=inv[b][:], in_=den[b][:])
 
-        def sigmoid_gate(first, last):
-            blocks = slice(first, last)
-            nc.scalar.activation(out=tanh_og[:, :, blocks, :], in_=og_sb[:, :, blocks, :], func=ACT.Tanh, scale=0.5)
-
-        def affine_gate(first, last):
-            blocks = slice(first, last)
-            nc.scalar.activation(out=gate_sb[:, :, blocks, :], in_=tanh_og[:, :, blocks, :], func=ACT.Copy, scale=0.5, bias=0.5)
-
         def finish(b):
             for h in range(HEADS):
                 nc.vector.scalar_tensor_tensor(
                     out=result[b][:, h, :],
                     in0=y[b][:, h, :],
                     scalar=inv[b][:, h : h + 1],
-                    in1=gate_sb[:, h, b, :],
+                    in1=gate[:, h, b, :],
                     op0=ALU.mult,
                     op1=ALU.mult,
                 )
-            nc.sync.dma_start(out=out[:, BLOCK * b : BLOCK * (b + 1), :].rearrange("h p e -> p h e"), in_=result[b][:])
+            nc.sync.dma_start(out=out[:, BLOCK * b : BLOCK * (b + 1), :].rearrange("h m e -> m h e"), in_=result[b][:])
 
-        round_keys(vector_round, 0, 0, 0, 128)
-        round_keys(scalar_round, 0, 1, 0, 128)
-        quantize_keys(0, 0)
-        quantize_keys(0, 1)
-        round_queries(vector_round, 0)
-        round_queries(scalar_round, 1)
-        round_queries(vector_round, 2)
-        round_queries(scalar_round, 3)
-        quantize_queries(0)
-        quantize_queries(1)
-        quantize_queries(2)
-        quantize_queries(3)
-        exp_scores(0, 0, 0)
-        exp_scores(0, 0, 1)
-        scale_mask(vector_scale, 0, 0, 0, 512)
-        scale_mask(vector_scale, 0, 1, 0, 512)
-        scale_mask(vector_scale, 0, 2, 0, 512)
-        scale_mask(vector_scale, 0, 3, 0, 512)
-        exp_scores(0, 1, 0)
-        exp_scores(0, 1, 1)
+
+        rounders = (vector_round, scalar_round)
+        for pair in range(2):
+            round_keys(rounders[pair], 0, pair)
+        for pair in range(2):
+            quantize_keys(0, pair)
+        for b in range(BLOCKS):
+            round_queries(rounders[b % 2], b)
+        for b in range(BLOCKS):
+            quantize_queries(b)
+        for r in range(PACK):
+            scale_mask(vector_scale if r else scalar_scale, 0, r)
+
+        exp_scores(0, 0)
+        exp_scores(0, 1)
+        exp_scores(0, 2)
         weigh(0, 0, 0, 1)
         weigh(0, 1, 0, 1)
-        exp_scores(0, 2, 0)
-        exp_scores(0, 2, 1)
         weigh(0, 0, 1, 1)
-        round_keys(scalar_round, 1, 1, 0, 128)
-        round_keys(vector_round, 1, 0, 0, 128)
+        for pair in range(2):
+            round_keys(rounders[pair], 1, pair)
         weigh(0, 1, 1, 1)
         quantize_keys(1, 0)
-        quantize_weights(0, 0, 0, 2)
-        quantize_weights(0, 1, 0, 2)
-        scale_mask(vector_scale, 1, 1, 0, 512)
+        for h in range(HEADS):
+            quantize_weights(0, h, 0, 2)
+        scale_mask(vector_scale, 1, 1)
         quantize_keys(1, 1)
-        exp_scores(0, 3, 0)
-        exp_scores(0, 3, 1)
-        scale_mask(scalar_scale, 1, 0, 0, 512)
-        scale_mask(vector_scale, 1, 2, 0, 512)
-        scale_mask(vector_scale, 1, 3, 0, 512)
+        exp_scores(0, 3)
+        scale_mask(scalar_scale, 1, 0)
+        scale_mask(vector_scale, 1, 2)
+        scale_mask(vector_scale, 1, 3)
+
+        exp_scores(1, 0)
+        exp_scores(1, 1)
+        for c in range(PASSES):
+            round_values(c)
+        exp_scores(1, 2)
+        exp_scores(1, 3)
         weigh(0, 0, 2, 2)
-        exp_scores(1, 0, 0)
-        exp_scores(1, 0, 1)
-        exp_scores(1, 1, 0)
-        exp_scores(1, 1, 1)
         weigh(0, 1, 2, 2)
         quantize_weights(0, 0, 2, 2)
-        round_values(0, 0)
-        round_values(0, 1)
         weigh(1, 0, 0, 2)
         quantize_weights(0, 1, 2, 2)
-        round_values(1, 0)
-        exp_scores(1, 2, 0)
-        exp_scores(1, 2, 1)
-        round_values(1, 1)
         weigh(1, 1, 0, 2)
         quantize_weights(1, 0, 0, 2)
         quantize_values(0)
-        exp_scores(1, 3, 0)
-        exp_scores(1, 3, 1)
         quantize_weights(1, 1, 0, 2)
-        sigmoid_gate(0, 2)
-        sigmoid_gate(2, 4)
-        affine_gate(0, 2)
-        affine_gate(2, 4)
+
+        halves = (slice(0, 2), slice(2, 4))
+        for half in halves:
+            nc.scalar.activation(out=tanh_og[:, :, half, :], in_=og_sb[:, :, half, :], func=ACT.Tanh, scale=0.5)
+        for half in halves:
+            nc.scalar.activation(out=gate[:, :, half, :], in_=tanh_og[:, :, half, :], func=ACT.Copy, scale=0.5, bias=0.5)
+
         weigh(1, 0, 2, 1)
         quantize_values(1)
-        second_product(0, 0)
-        second_product(0, 1)
-        second_product(1, 0)
-        second_product(1, 1)
+        for b in range(2):
+            for h in range(HEADS):
+                second_product(b, h)
         weigh(1, 1, 2, 1)
         quantize_weights(1, 0, 2, 1)
         second_product(2, 0)

from contextlib import ExitStack

import concourse.mybir as mybir

HEADS, FEATURES, QUERIES, TOKENS, VALUES = 2, 256, 512, 1024, 128
FLOPS = 2 * HEADS * TOKENS * QUERIES * (FEATURES + VALUES)

F32 = mybir.dt.float32
BF16 = mybir.dt.bfloat16
U32 = mybir.dt.uint32
U8 = mybir.dt.uint8
FP8X4 = mybir.dt.float8_e4m3fn_x4
ACT = mybir.ActivationFunctionType
ALU = mybir.AluOpType

P = 128
PACK = 4
ROWS = FEATURES // PACK
PASS = P * PACK
PASSES = TOKENS // PASS
BLOCK = 128
BLOCKS = QUERIES // BLOCK
RUN = 2


def tile_rows_a_exp_mask_sink_gate_kernel(tc, qT, kT, t, v, mask, sink, og, out):
    nc = tc.nc
    with ExitStack() as ctx:
        sbuf = ctx.enter_context(tc.tile_pool(name="sbuf", bufs=1))
        score_pool = [ctx.enter_context(tc.psum_pool(name="scores%d" % h, bufs=2)) for h in range(HEADS)]
        y_pool = ctx.enter_context(tc.psum_pool(name="y", bufs=1))
        ctx.enter_context(nc.allow_non_contiguous_dma(reason="one sink for each partition, head and block"))
        ctx.enter_context(tc.manual_schedule())

        def tiles(name, count, shape, dtype):
            return [sbuf.tile(shape, dtype, name="%s%d" % (name, n), align_bytes=64) for n in range(count)]

        def mx_tiles(name, count, words):
            codes = tiles(name + "_codes", count, [P, words], U32)
            scales = tiles(name + "_scales", count, [P, words], U8)
            return list(zip(codes, scales))

        def window(operand, rows, first, count):
            return operand[0][rows, first : first + count], operand[1][rows, first : first + count]

        def quantize(operand, source):
            nc.vector.quantize_mx(out=operand[0].bitcast(FP8X4), scales=operand[1], in_=source)

        def product(dst, stationary, moving, start, stop):
            nc.tensor.matmul_mx(
                out=dst,
                lhsT=stationary[0].bitcast(FP8X4),
                lhsT_scale=stationary[1],
                rhs=moving[0].bitcast(FP8X4),
                rhs_scale=moving[1],
                start=start,
                stop=stop,
            )

        def vector_round(dst, src):
            nc.vector.tensor_copy(out=dst, in_=src)

        def scalar_round(dst, src):
            nc.scalar.activation(out=dst, in_=src, func=ACT.Copy)

        def vector_scale(dst, src, factor):
            nc.vector.tensor_scalar(out=dst, in0=src, scalar1=factor, scalar2=None, op0=ALU.mult)

        def scalar_scale(dst, src, factor):
            nc.scalar.activation(out=dst, in_=src, func=ACT.Copy, scale=factor)

        everywhere = slice(0, P)
        t_sb = tiles("t", 1, [P, PASSES, PACK], F32)[0]
        q_raw = tiles("q_raw", 1, [P, PACK, QUERIES], F32)[0]
        k_raw = tiles("k_raw", PASSES, [P, PACK, PASS], F32)
        mask_early = tiles("mask_early", PASSES, [P, PACK - 1, QUERIES], F32)
        mask_late = tiles("mask_late", PASSES, [P, QUERIES], F32)
        v_raw = tiles("v_raw", PASSES, [P, HEADS, PACK * VALUES], F32)
        og_sb = tiles("og", 1, [P, HEADS, BLOCKS, VALUES], F32)[0]
        sink_sb = tiles("sink", 1, [P, HEADS, BLOCKS], F32)[0]

        q_rows = qT.rearrange("h (p j) q -> (h p) j q", j=PACK)
        k_rows = kT.rearrange("h (p j) n -> (h p) j n", j=PACK)
        mask_rows = mask.rearrange("(c s r) q -> c s r q", c=PASSES, r=PACK)
        v_rows = v.rearrange("h (c s r) e -> c s h (r e)", c=PASSES, r=PACK)
        nc.scalar.dma_start(out=t_sb[:], in_=t.rearrange("(c s r) o -> s c (r o)", c=PASSES, r=PACK))
        for c in range(PASSES):
            nc.sync.dma_start(out=k_raw[c][:], in_=k_rows[:, :, PASS * c : PASS * (c + 1)])
            if c == 0:
                nc.sync.dma_start(out=q_raw[:], in_=q_rows)
            nc.sync.dma_start(out=mask_early[c][:], in_=mask_rows[c][:, 0 : PACK - 1, :])
            nc.sync.dma_start(out=mask_late[c][:], in_=mask_rows[c][:, PACK - 1, :])
        for c in range(PASSES):
            nc.sync.dma_start(out=v_raw[c][:], in_=v_rows[c])
        nc.sync.dma_start(
            out=og_sb[:].rearrange("m h b e -> m (h b) e"), in_=og.rearrange("h (b m) e -> m (h b) e", m=BLOCK)
        )
        nc.sync.dma_start(out=sink_sb[:], in_=sink.rearrange("h (b m) o -> m h (b o)", m=BLOCK))

        k_bf = [tiles("k_bf%d_" % c, 2, [P, 2, P, PACK], BF16) for c in range(PASSES)]
        k_mx = [mx_tiles("k%d_" % c, 2, 2 * P) for c in range(PASSES)]
        q_bf = tiles("q_bf", BLOCKS, [P, BLOCK, PACK], BF16)
        q_mx = mx_tiles("q", BLOCKS, BLOCK)
        v_bf = tiles("v_bf", PASSES, [P, HEADS, VALUES, PACK], BF16)
        v_mx = mx_tiles("v", PASSES, HEADS * VALUES)
        mask_t = tiles("mask_t", PASSES, [P, PACK, QUERIES], F32)
        p_sb = [[tiles("p%d%d_" % (c, h), 2, [P, 2 * PASS], F32) for h in range(HEADS)] for c in range(PASSES)]
        w_bf = [[tiles("w%d%d_" % (c, h), 2, [P, 2 * PASS], BF16) for h in range(HEADS)] for c in range(PASSES)]
        w_mx = [[mx_tiles("w%d%d_" % (c, h), 2, 2 * BLOCK) for h in range(HEADS)] for c in range(PASSES)]
        tanh_og = tiles("tanh_og", 1, [P, HEADS, BLOCKS, VALUES], F32)[0]
        gate = tiles("gate", 1, [P, HEADS, BLOCKS, VALUES], F32)[0]
        den = tiles("den", BLOCKS, [P, HEADS], F32)
        inv = tiles("inv", BLOCKS, [P, HEADS], F32)
        result = tiles("result", BLOCKS, [P, HEADS, VALUES], F32)
        y = [y_pool.tile([P, HEADS, VALUES], F32, name="y%d" % b) for b in range(BLOCKS)]

        def round_keys(rounder, c, pair):
            src = k_raw[c][:].rearrange("p j (s r) -> p s j r", r=PACK)[:, :, :, 2 * pair : 2 * pair + 2]
            rounder(k_bf[c][pair][:].rearrange("p r s j -> p s j r"), src)

        def quantize_keys(c, pair):
            quantize(window(k_mx[c][pair], everywhere, 0, 2 * P), k_bf[c][pair][:].rearrange("p r s j -> p (r s j)"))

        def round_queries(rounder, b):
            src = q_raw[:, :, BLOCK * b : BLOCK * (b + 1)].rearrange("p j (n i) -> p n j i", i=RUN)
            rounder(q_bf[b][:].rearrange("p (n i) j -> p n j i", i=RUN), src)

        def quantize_queries(b):
            quantize(window(q_mx[b], everywhere, 0, BLOCK), q_bf[b][:].rearrange("p q j -> p (q j)"))

        def round_values(c):
            src = v_raw[c][:].rearrange("s h (r n i) -> s h n r i", r=PACK, i=RUN)
            nc.scalar.copy(out=v_bf[c][:].rearrange("s h (n i) r -> s h n r i", i=RUN), in_=src)

        def quantize_values(c):
            quantize(window(v_mx[c], everywhere, 0, HEADS * VALUES), v_bf[c][:].rearrange("s h e r -> s (h e r)"))

        def scale_mask(scaler, c, r):
            src = mask_early[c][:, r, :] if r < PACK - 1 else mask_late[c][:]
            scaler(mask_t[c][:, r, :], src, t_sb[:, c, r : r + 1])

        def exp_scores(c, b):
            banks = [score_pool[h].tile([P, PACK, BLOCK], F32, name="scores%d" % h) for h in range(HEADS)]
            for r in range(PACK):
                for h in range(HEADS):
                    rows = slice(ROWS * h, ROWS * (h + 1))
                    keys = window(k_mx[c][r // 2], rows, P * (r % 2), P)
                    product(banks[h][:, r, :], keys, window(q_mx[b], rows, 0, BLOCK), True, True)
            for h in range(HEADS):
                dst = p_sb[c][h][b // 2][:, PASS * (b % 2) : PASS * (b % 2 + 1)]
                nc.scalar.activation(
                    out=dst.rearrange("s (n r i) -> s n r i", r=PACK, i=RUN),
                    in_=banks[h][:].rearrange("s r (n i) -> s n r i", i=RUN),
                    func=ACT.Exp,
                )

        def weigh(c, h, b, count):
            cols = slice(PASS * (b % 2), PASS * (b % 2 + count))
            nc.vector.tensor_tensor(
                out=w_bf[c][h][b // 2][:, cols].rearrange("s (n i r) -> s n r i", r=PACK, i=RUN),
                in0=p_sb[c][h][b // 2][:, cols].rearrange("s (n r i) -> s n r i", r=PACK, i=RUN),
                in1=mask_t[c][:, :, BLOCK * b : BLOCK * (b + count)].rearrange("s r (n i) -> s n r i", i=RUN),
                op=ALU.mult,
            )

        def quantize_weights(c, h, b, count):
            operand = window(w_mx[c][h][b // 2], everywhere, BLOCK * (b % 2), BLOCK * count)
            quantize(operand, w_bf[c][h][b // 2][:, PASS * (b % 2) : PASS * (b % 2 + count)])

        def second_product(b, h):
            for c in range(PASSES):
                weights = window(w_mx[c][h][b // 2], everywhere, BLOCK * (b % 2), BLOCK)
                values = window(v_mx[c], everywhere, VALUES * h, VALUES)
                product(y[b][:, h, :], weights, values, c == 0, c == PASSES - 1)

        def denominators(b):
            nc.vector.tensor_tensor(out=den[b][:], in0=y[b][:, :, VALUES - 1], in1=sink_sb[:, :, b], op=ALU.add)

        def invert(b):
            nc.vector.reciprocal(out=inv[b][:], in_=den[b][:])

        def finish(b):
            for h in range(HEADS):
                nc.vector.scalar_tensor_tensor(
                    out=result[b][:, h, :],
                    in0=y[b][:, h, :],
                    scalar=inv[b][:, h : h + 1],
                    in1=gate[:, h, b, :],
                    op0=ALU.mult,
                    op1=ALU.mult,
                )
            nc.sync.dma_start(out=out[:, BLOCK * b : BLOCK * (b + 1), :].rearrange("h m e -> m h e"), in_=result[b][:])


        rounders = (vector_round, scalar_round)
        for pair in range(2):
            round_keys(rounders[pair], 0, pair)
        for pair in range(2):
            quantize_keys(0, pair)
        for b in range(BLOCKS):
            round_queries(rounders[b % 2], b)
        for b in range(BLOCKS):
            quantize_queries(b)
        for r in range(PACK):
            scale_mask(vector_scale if r else scalar_scale, 0, r)

        exp_scores(0, 0)
        exp_scores(0, 1)
        exp_scores(0, 2)
        weigh(0, 0, 0, 1)
        weigh(0, 1, 0, 1)
        weigh(0, 0, 1, 1)
        for pair in range(2):
            round_keys(rounders[pair], 1, pair)
        weigh(0, 1, 1, 1)
        quantize_keys(1, 0)
        for h in range(HEADS):
            quantize_weights(0, h, 0, 2)
        scale_mask(vector_scale, 1, 1)
        quantize_keys(1, 1)
        exp_scores(0, 3)
        scale_mask(scalar_scale, 1, 0)
        scale_mask(vector_scale, 1, 2)
        scale_mask(vector_scale, 1, 3)

        exp_scores(1, 0)
        exp_scores(1, 1)
        for c in range(PASSES):
            round_values(c)
        exp_scores(1, 2)
        exp_scores(1, 3)
        weigh(0, 0, 2, 2)
        weigh(0, 1, 2, 2)
        quantize_weights(0, 0, 2, 2)
        weigh(1, 0, 0, 2)
        quantize_weights(0, 1, 2, 2)
        weigh(1, 1, 0, 2)
        quantize_weights(1, 0, 0, 2)
        quantize_values(0)
        quantize_weights(1, 1, 0, 2)

        halves = (slice(0, 2), slice(2, 4))
        for half in halves:
            nc.scalar.activation(out=tanh_og[:, :, half, :], in_=og_sb[:, :, half, :], func=ACT.Tanh, scale=0.5)
        for half in halves:
            nc.scalar.activation(out=gate[:, :, half, :], in_=tanh_og[:, :, half, :], func=ACT.Copy, scale=0.5, bias=0.5)

        weigh(1, 0, 2, 1)
        quantize_values(1)
        for b in range(2):
            for h in range(HEADS):
                second_product(b, h)
        weigh(1, 1, 2, 1)
        quantize_weights(1, 0, 2, 1)
        second_product(2, 0)
        weigh(1, 0, 3, 1)
        quantize_weights(1, 1, 2, 1)
        second_product(2, 1)
        denominators(0)
        denominators(1)
        weigh(1, 1, 3, 1)
        quantize_weights(1, 0, 3, 1)
        second_product(3, 0)
        invert(0)
        invert(1)
        denominators(2)
        quantize_weights(1, 1, 3, 1)
        second_product(3, 1)
        invert(2)
        finish(0)
        denominators(3)
        finish(1)
        invert(3)
        finish(2)
        finish(3)
